import numpy as np
import ml_dtypes

BF16 = ml_dtypes.bfloat16


def bf(x):
    return np.asarray(x, np.float32).astype(BF16)


def f32(x):
    return np.asarray(x, np.float32)


def f64(x):
    return np.asarray(x).astype(np.float64)


def striped(idx):
    return np.tile(idx.reshape(-1, 16).T, (8, 1))


S, K, M, N, E, Q = 512, 128, 128, 256, 2, 128


def setup_inputs():
    return {"base": bf(np.random.standard_normal((M, S))), "x": bf(np.random.standard_normal((K, N))), "w": bf(np.random.standard_normal((E, K, M)) / np.sqrt(K)), "offs": striped(np.random.permutation(S)[:N])}


def reference(base, x, w, offs):
    idx = offs[:16].T.reshape(-1)
    z = f64(base).copy()
    for e in range(E):
        z[:, idx[e * Q : (e + 1) * Q]] = f64(w)[e].T @ f64(x)[:, e * Q : (e + 1) * Q]
    return z

@@ -1,0 +1,51 @@
+import concourse.mybir as mybir
+from concourse.masks import make_identity
+
+BF16 = mybir.dt.bfloat16
+F32 = mybir.dt.float32
+U16 = mybir.dt.uint16
+
+P = 128
+TOKENS = 512
+EXPERTS = 2
+PIECE = 128
+ENTRIES = EXPERTS * PIECE
+LANES = 16
+
+FLOPS = 2 * P * P * ENTRIES
+
+
+def tile_scatter_matmul_kernel(tc, base, x, w, offs, out):
+    nc = tc.nc
+    with (
+        tc.tile_pool(name="held", bufs=1) as held,
+        tc.psum_pool(name="psum", bufs=1) as psum,
+    ):
+        base_tile = held.tile([P, TOKENS], BF16, name="base_tile")
+        offsets = held.tile([P, ENTRIES // LANES], U16, name="offsets")
+        x_tile = held.tile([P, ENTRIES], BF16, name="x_tile")
+        w_tile = held.tile([P, EXPERTS, P], BF16, name="w_tile")
+        identity = held.tile([P, P], BF16, name="identity")
+        z_tile = held.tile([P, TOKENS], F32, name="z_tile")
+        window = psum.tile([P, TOKENS], F32, name="window")
+
+        nc.sync.dma_start(base_tile[:], base)
+        nc.sync.dma_start(w_tile[:], w.rearrange("e k m -> k e m"))
+        nc.sync.dma_start(x_tile[:], x)
+        nc.sync.dma_start(offsets[:], offs)
+
+        make_identity(nc, identity[:])
+        nc.tensor.matmul(window[:], identity[:], base_tile[:], start=True, stop=True)
+
+        columns = PIECE // LANES
+        for e in range(EXPERTS):
+            nc.tensor.matmul(
+                window[:].indirect(offsets[:, e * columns : (e + 1) * columns]),
+                w_tile[:, e, :],
+                x_tile[:, e * PIECE : (e + 1) * PIECE],
+                start=True,
+                stop=True,
+            )
+
+        nc.vector.tensor_copy(z_tile[:], window[:])
+        nc.sync.dma_start(out, z_tile[:])

@@ -12,6 +12,8 @@ PIECE = 128
 ENTRIES = EXPERTS * PIECE
 LANES = 16
 
+WARM_UPS = 4
+
 FLOPS = 2 * P * P * ENTRIES
 
 
@@ -27,12 +29,18 @@ def tile_scatter_matmul_kernel(tc, base, x, w, offs, out):
         w_tile = held.tile([P, EXPERTS, P], BF16, name="w_tile")
         identity = held.tile([P, P], BF16, name="identity")
         z_tile = held.tile([P, TOKENS], F32, name="z_tile")
+        zeros = held.tile([P, TOKENS], BF16, name="zeros")
         window = psum.tile([P, TOKENS], F32, name="window")
+        warm_bank = psum.tile([P, TOKENS], F32, name="warm_bank")
 
         nc.sync.dma_start(base_tile[:], base)
         nc.sync.dma_start(w_tile[:], w.rearrange("e k m -> k e m"))
         nc.sync.dma_start(x_tile[:], x)
         nc.sync.dma_start(offsets[:], offs)
+
+        nc.vector.memset(zeros[:], 0.0)
+        for i in range(WARM_UPS):
+            nc.tensor.matmul(warm_bank[:], zeros[:, :P], zeros[:], start=True, stop=True)
 
         make_identity(nc, identity[:])
         nc.tensor.matmul(window[:], identity[:], base_tile[:], start=True, stop=True)

@@ -12,7 +12,7 @@ PIECE = 128
 ENTRIES = EXPERTS * PIECE
 LANES = 16
 
-WARM_UPS = 4
+WARM_UPS = 3
 
 FLOPS = 2 * P * P * ENTRIES
 
@@ -29,7 +29,7 @@ def tile_scatter_matmul_kernel(tc, base, x, w, offs, out):
         w_tile = held.tile([P, EXPERTS, P], BF16, name="w_tile")
         identity = held.tile([P, P], BF16, name="identity")
         z_tile = held.tile([P, TOKENS], F32, name="z_tile")
-        zeros = held.tile([P, TOKENS], BF16, name="zeros")
+        zeros = held.tile([P, P], BF16, name="zeros")
         window = psum.tile([P, TOKENS], F32, name="window")
         warm_bank = psum.tile([P, TOKENS], F32, name="warm_bank")
 
@@ -39,8 +39,9 @@ def tile_scatter_matmul_kernel(tc, base, x, w, offs, out):
         nc.sync.dma_start(offsets[:], offs)
 
         nc.vector.memset(zeros[:], 0.0)
+        zeros_row = zeros[:].unsqueeze(1).to_broadcast([P, TOKENS // P, P])
         for i in range(WARM_UPS):
-            nc.tensor.matmul(warm_bank[:], zeros[:, :P], zeros[:], start=True, stop=True)
+            nc.tensor.matmul(warm_bank[:], zeros[:], zeros_row, start=True, stop=True)
 
         make_identity(nc, identity[:])
         nc.tensor.matmul(window[:], identity[:], base_tile[:], start=True, stop=True)

@@ -34,7 +34,7 @@ def tile_scatter_matmul_kernel(tc, base, x, w, offs, out):
         warm_bank = psum.tile([P, TOKENS], F32, name="warm_bank")
 
         nc.sync.dma_start(base_tile[:], base)
-        nc.sync.dma_start(w_tile[:], w.rearrange("e k m -> k e m"))
+        nc.scalar.dma_start(w_tile[:], w.rearrange("e k m -> k e m"))
         nc.sync.dma_start(x_tile[:], x)
         nc.sync.dma_start(offsets[:], offs)
 

import concourse.mybir as mybir
from concourse.masks import make_identity

BF16 = mybir.dt.bfloat16
F32 = mybir.dt.float32
U16 = mybir.dt.uint16

P = 128
TOKENS = 512
EXPERTS = 2
PIECE = 128
ENTRIES = EXPERTS * PIECE
LANES = 16

WARM_UPS = 3

FLOPS = 2 * P * P * ENTRIES


def tile_scatter_matmul_kernel(tc, base, x, w, offs, out):
    nc = tc.nc
    with (
        tc.tile_pool(name="held", bufs=1) as held,
        tc.psum_pool(name="psum", bufs=1) as psum,
    ):
        base_tile = held.tile([P, TOKENS], BF16, name="base_tile")
        offsets = held.tile([P, ENTRIES // LANES], U16, name="offsets")
        x_tile = held.tile([P, ENTRIES], BF16, name="x_tile")
        w_tile = held.tile([P, EXPERTS, P], BF16, name="w_tile")
        identity = held.tile([P, P], BF16, name="identity")
        z_tile = held.tile([P, TOKENS], F32, name="z_tile")
        zeros = held.tile([P, P], BF16, name="zeros")
        window = psum.tile([P, TOKENS], F32, name="window")
        warm_bank = psum.tile([P, TOKENS], F32, name="warm_bank")

        nc.sync.dma_start(base_tile[:], base)
        nc.scalar.dma_start(w_tile[:], w.rearrange("e k m -> k e m"))
        nc.sync.dma_start(x_tile[:], x)
        nc.sync.dma_start(offsets[:], offs)

        nc.vector.memset(zeros[:], 0.0)
        zeros_row = zeros[:].unsqueeze(1).to_broadcast([P, TOKENS // P, P])
        for i in range(WARM_UPS):
            nc.tensor.matmul(warm_bank[:], zeros[:], zeros_row, start=True, stop=True)

        make_identity(nc, identity[:])
        nc.tensor.matmul(window[:], identity[:], base_tile[:], start=True, stop=True)

        columns = PIECE // LANES
        for e in range(EXPERTS):
            nc.tensor.matmul(
                window[:].indirect(offsets[:, e * columns : (e + 1) * columns]),
                w_tile[:, e, :],
                x_tile[:, e * PIECE : (e + 1) * PIECE],
                start=True,
                stop=True,
            )

        nc.vector.tensor_copy(z_tile[:], window[:])
        nc.sync.dma_start(out, z_tile[:])
